import numpy as np
import ml_dtypes


def mxq(x, axis, fmt="e4m3"):
    dtype, down = {"e4m3": (ml_dtypes.float8_e4m3fn, 7), "e5m2": (ml_dtypes.float8_e5m2, 14)}[fmt]
    v = np.moveaxis(np.asarray(x, np.float32).astype(ml_dtypes.bfloat16).astype(np.float64), axis, -1)
    blocks = v.reshape(v.shape[:-1] + (-1, 32))
    amax = np.abs(blocks).max(-1, keepdims=True)
    byte = np.maximum(np.where(amax > 0, np.frexp(amax)[1] - 1 + 127, 0) - down, 1)
    scale = np.exp2(byte - 127.0)
    codes = (blocks / scale).astype(np.float32).astype(dtype).astype(np.float64)
    return np.moveaxis((codes * scale).reshape(v.shape), -1, axis)


WIDE = False


def mx_kscale(k):
    if not WIDE:
        return np.ones(k)
    levels = np.array([10, -10, 5, -5, 0])
    if k % 512:
        return np.exp2(np.random.permutation(np.resize(levels, k // 32))).repeat(32)
    a = np.empty((k // 512, 16))
    for p in range(k // 512):
        a[p, :8] = np.random.permutation(np.resize(levels, 8))
        for g in range(8):
            far = levels[np.abs(levels - a[p, g]) >= 10]
            a[p, g + 8] = far[np.random.randint(len(far))]
    return np.exp2(a.ravel()).repeat(32)


BF16 = ml_dtypes.bfloat16


def bf(x):
    return np.asarray(x, np.float32).astype(BF16)


def f64(x):
    return np.asarray(x).astype(np.float64)


E2M1 = np.array([0.0, 0.5, 1.0, 1.5, 2.0, 3.0, 4.0, 6.0, -0.0, -0.5, -1.0, -1.5, -2.0, -3.0, -4.0, -6.0])


def pack_weight(w, fmt):
    k, n = w.shape
    w = f64(bf(w)).reshape(k // 32, 32, n)
    amax = np.abs(w).max(1)
    if fmt == "e4m3":
        byte = np.frexp(amax)[1] - 1 + 127 - 7
    else:
        mant, ex = np.frexp(amax / 6.0)
        byte = np.where(mant > 0.5, ex, ex - 1) + 127
    byte = np.clip(np.where(amax > 0, byte, 1), 1, 254)
    scaled = (w * np.exp2(127.0 - byte)[:, None, :]).reshape(k, n).astype(np.float32)
    by_word = np.ascontiguousarray(scaled.reshape(k // 512, 128, 4, n).transpose(0, 1, 3, 2))
    if fmt == "e4m3":
        words = by_word.astype(ml_dtypes.float8_e4m3fn).view(np.uint8)
    else:
        c = by_word.astype(ml_dtypes.float4_e2m1fn).view(np.uint8) & 0xF
        words = c[..., 0::2] | (c[..., 1::2] << 4)
    return np.ascontiguousarray(words), np.ascontiguousarray(byte.astype(np.uint8).reshape(k // 512, 16, n))


def unpack_weight(words, scales, fmt):
    g, p, n, _ = words.shape
    if fmt == "e4m3":
        vals = np.ascontiguousarray(words).view(ml_dtypes.float8_e4m3fn).astype(np.float64)
    else:
        nib = np.empty((g, p, n, 4), np.uint8)
        nib[..., 0::2] = words & 0xF
        nib[..., 1::2] = words >> 4
        vals = E2M1[nib]
    vals = vals * np.repeat(np.exp2(scales.astype(np.float64) - 127.0), 8, axis=1)[..., None]
    return vals.transpose(0, 1, 3, 2).reshape(g * 512, n)
def pack4(w):
    words, scales = pack_weight(w, "e2m1")
    return words.reshape(words.shape[0], 128, -1), scales


def unpack4(words, scales):
    return unpack_weight(words.reshape(words.shape[0], 128, -1, 2), scales, "e2m1")


H, T, P = 1024, 1536, 512

CORR = 0.35


def setup_inputs():
    s, u = mx_kscale(T), mx_kscale(H)
    feed = CORR * np.random.standard_normal((T, T)) / np.sqrt(T)
    share = CORR * np.abs(np.random.standard_normal((H, H))) / np.sqrt(H)
    inhib = np.random.standard_normal((T, P)) / np.sqrt(T)
    feed_words, feed_scales = pack4(feed / s[:, None] * s)
    share_words, share_scales = pack4(share / u[:, None] * u)
    inhib_words, inhib_scales = pack4(inhib / s[:, None])
    return {"x": bf(np.random.standard_normal((H, T)) * s * u[:, None]),
            "feed_words": feed_words, "feed_scales": feed_scales,
            "uptake": bf(np.random.uniform(0.5, 1.5, T)),
            "share_words": share_words, "share_scales": share_scales,
            "inhib_words": inhib_words, "inhib_scales": inhib_scales,
            "gate": bf(np.random.uniform(0.2, 1.0, (H, P)) / u[:, None]),
            "rate": bf(0.5 * np.random.standard_normal(P))}


def reference(x, feed_words, feed_scales, uptake, share_words, share_scales, inhib_words, inhib_scales, gate, rate):
    x = f64(x)
    fed = mxq(x, 1, "e4m3") @ unpack4(feed_words, feed_scales)
    y = x + f64(uptake) * fed
    shared = unpack4(share_words, share_scales).T @ mxq(y, 0, "e4m3")
    z = y + shared
    press = mxq(z, 1, "e4m3") @ unpack4(inhib_words, inhib_scales)
    return f64(rate) - f64(gate) * press

@@ -1,0 +1,323 @@
+from contextlib import ExitStack
+
+import concourse.mybir as mybir
+from concourse.masks import make_identity
+
+HOSTS, TAXA, MON = 1024, 1536, 512
+FLOPS = 2 * HOSTS * TAXA * TAXA + 2 * HOSTS * HOSTS * TAXA + 2 * HOSTS * TAXA * MON
+
+F32 = mybir.dt.float32
+BF16 = mybir.dt.bfloat16
+U32 = mybir.dt.uint32
+I32 = mybir.dt.int32
+U8 = mybir.dt.uint8
+E4M3 = mybir.dt.float8_e4m3fn_x4
+E2M1 = mybir.dt.float4_e2m1fn_x4
+ADD = mybir.AluOpType.add
+MULT = mybir.AluOpType.mult
+SUB = mybir.AluOpType.subtract
+
+P = 128
+K_PASS = 512
+TG = TAXA // K_PASS
+HG = HOSTS // K_PASS
+HB = HOSTS // P
+
+
+def tile_microbiome_gated_growth_t2_kernel(
+    tc, x, feed_words, feed_scales, uptake, share_words, share_scales, inhib_words, inhib_scales, gate, rate, out
+):
+    nc = tc.nc
+    with ExitStack() as ctx:
+        keep = ctx.enter_context(tc.tile_pool(name="keep", bufs=1))
+        ring = ctx.enter_context(tc.tile_pool(name="ring", bufs=2))
+        psum = ctx.enter_context(tc.psum_pool(name="psum", bufs=4))
+        ctx.enter_context(tc.manual_schedule())
+
+        a_scale_in = keep.tile([P, TG, TAXA], U8, align_bytes=64)
+        c_scale = keep.tile([P, HG, HOSTS], U8, align_bytes=64)
+        b_scale = keep.tile([P, TG, MON], U8, align_bytes=64)
+        ident = keep.tile([P, P], F32)
+        nc.vector.memset(a_scale_in[:].rearrange("p k n -> p (k n)").bitcast(I32), 0)
+        make_identity(nc, ident[:])
+        nc.gpsimd.memset(c_scale[:].rearrange("p k n -> p (k n)").bitcast(I32), 0)
+        nc.gpsimd.memset(b_scale[:].rearrange("p k n -> p (k n)").bitcast(I32), 0)
+
+        x_in = {}
+        a_in = [keep.tile([P, TG, 2 * K_PASS], U8, name=f"a_in{g}", align_bytes=64) for g in range(TG)]
+        c_codes = keep.tile([P, HG, 2 * HOSTS], U8, align_bytes=64)
+        b_codes = keep.tile([P, TG, 2 * MON], U8, align_bytes=64)
+        u = keep.tile([P, TG, 4], BF16, align_bytes=64)
+        gates = keep.tile([P, HB, MON], BF16, align_bytes=64)
+        rates = keep.tile([P, MON], BF16, align_bytes=64)
+
+        def load_x(i):
+            x_in[i] = ring.tile([P, TAXA], BF16, tag="x_in", bufs=6, name="x_in", align_bytes=64)
+            nc.sync.dma_start(out=x_in[i][:], in_=x[i * P : (i + 1) * P, :])
+
+        def load_a(g):
+            cols = slice(2 * K_PASS * g, 2 * K_PASS * (g + 1))
+            nc.sync.dma_start(
+                out=a_in[g][:].bitcast(I32), in_=feed_words[:, :, cols].rearrange("k p b -> p k b").bitcast(I32)
+            )
+
+        def load_scales(plane, rows):
+            for q in range(4):
+                nc.sync.dma_start(
+                    out=plane[32 * q : 32 * q + 4, :, :].bitcast(I32),
+                    in_=rows[:, 4 * q : 4 * q + 4, :].rearrange("k q n -> q k n").bitcast(I32),
+                )
+
+        load_x(0)
+        load_a(0)
+        load_x(1)
+        load_scales(a_scale_in, feed_scales)
+        for i in range(2, 6):
+            load_x(i)
+        nc.sync.dma_start(out=u[:], in_=uptake.rearrange("(g p t) -> p g t", g=TG, t=4))
+        load_a(1)
+        load_x(6)
+        load_x(7)
+        load_a(2)
+        nc.sync.dma_start(out=c_codes[:].bitcast(I32), in_=share_words.rearrange("k p b -> p k b").bitcast(I32))
+        load_scales(c_scale, share_scales)
+        nc.sync.dma_start(out=b_codes[:].bitcast(I32), in_=inhib_words.rearrange("k p b -> p k b").bitcast(I32))
+        load_scales(b_scale, inhib_scales)
+        nc.sync.dma_start(out=gates[:], in_=gate.rearrange("(c p) n -> p c n", p=P))
+        nc.sync.dma_start(out=rates[:], in_=rate.partition_broadcast(P))
+
+        xt = [keep.tile([P, TG, K_PASS, 4], BF16, name=f"xt{h}", align_bytes=64) for h in range(HG)]
+        x_codes = [keep.tile([P, TG, K_PASS], U32, name=f"x_codes{h}", align_bytes=64) for h in range(HG)]
+        x_scale = [keep.tile([P, TG, K_PASS], U8, name=f"x_scale{h}", align_bytes=64) for h in range(HG)]
+        a_codes = [keep.tile([P, TG, 2 * K_PASS], U8, name=f"a_codes{g}", align_bytes=64) for g in range(TG)]
+        a_scale = [keep.tile([P, TG, K_PASS], U8, name=f"a_scale{g}", align_bytes=64) for g in range(TG)]
+        y = [keep.tile([P, 4, HOSTS], F32, name=f"y{g}", align_bytes=64) for g in range(TG)]
+        z_codes = [keep.tile([P, HOSTS], U32, name=f"z_codes{g}", align_bytes=64) for g in range(TG)]
+        z_scale = [keep.tile([P, HOSTS], U8, name=f"z_scale{g}", align_bytes=64) for g in range(TG)]
+        y_codes, y_scale, y_round = {}, {}, {}
+        z_pair = {}
+
+        queue = []
+
+        def side():
+            if queue:
+                piece = queue[0]
+                queue.remove(piece)
+                piece[0](*piece[1:])
+
+        def flush():
+            while queue:
+                side()
+
+        def permute_codes(g, k):
+            nc.vector.tensor_copy(
+                out=a_codes[g][:, k, :].rearrange("p (t m b) -> p t m b", t=4, b=2),
+                in_=a_in[g][:, k, :].rearrange("p (m t b) -> p t m b", t=4, b=2),
+            )
+
+        def permute_scales(g, k):
+            nc.vector.tensor_copy(
+                out=a_scale[g][:, k, :].rearrange("p (t m) -> p t m", t=4),
+                in_=a_scale_in[:, k, K_PASS * g : K_PASS * (g + 1)].rearrange("p (m t) -> p t m", t=4),
+            )
+
+        def queue_permute(g):
+            for k in range(TG):
+                queue.append((permute_codes, g, k))
+            for k in range(TG):
+                queue.append((permute_scales, g, k))
+
+        def copy_out(engine, out, in_):
+            if engine == "S":
+                nc.scalar.copy(out=out, in_=in_)
+            else:
+                nc.vector.tensor_copy(out=out, in_=in_)
+
+        def transpose_x_pair(j, engines):
+            h, base = j // 2, 256 * (j % 2)
+            last = psum.tile([P, 4, P], F32, tag="tr", bufs=3, name="tr_last")
+            for i in range(2):
+                words = x_in[2 * j + i][:].bitcast(F32)
+                first = psum.tile([P, 4, P], F32, tag="tr", bufs=3, name="tr_first")
+                for k in range(TG):
+                    for s in range(2):
+                        dst = first[:, 2 * k + s, :] if k < 2 else last[:, 2 * i + s, :]
+                        nc.tensor.transpose(dst, words[:, 256 * k + s : 256 * (k + 1) : 2], ident[:])
+                cols = slice(base + P * i, base + P * (i + 1))
+                copy_out(
+                    engines[i],
+                    out=xt[h][:, 0:2, cols, :].rearrange("p k m e -> p k (m e)").bitcast(F32).rearrange("p k (m s) -> p k m s", s=2),
+                    in_=first[:].rearrange("p (k s) m -> p k m s", s=2),
+                )
+            copy_out(
+                engines[2],
+                out=xt[h][:, 2, base : base + 256, :].rearrange("p m e -> p (m e)").bitcast(F32).rearrange("p (i m s) -> p i m s", i=2, s=2),
+                in_=last[:].rearrange("p (i s) m -> p i m s", s=2),
+            )
+
+        def quantize_x(j, k):
+            h, base = j // 2, 256 * (j % 2)
+            cols = slice(base, base + 256)
+            nc.vector.quantize_mx(
+                out=x_codes[h][:, k, cols].bitcast(E4M3),
+                scales=x_scale[h][:, k, cols],
+                in_=xt[h][:, k, cols, :].rearrange("p m e -> p (m e)"),
+            )
+
+        def stage_one(g, h, tiles=range(4)):
+            if 0 in tiles:
+                y_round[g, h] = ring.tile([P, 4, K_PASS], BF16, tag="y_round", bufs=3, name="y_round", align_bytes=64)
+            hosts = slice(K_PASS * h, K_PASS * (h + 1))
+            for t in tiles:
+                fed = psum.tile([P, K_PASS], F32, tag="mm", bufs=5, name="fed")
+                for k in range(TG):
+                    nc.tensor.matmul_mx(
+                        out=fed[:],
+                        lhsT=a_codes[g][:, k, 256 * t : 256 * (t + 1)].bitcast(E2M1),
+                        lhsT_scale=a_scale[g][:, k, P * t : P * (t + 1)],
+                        rhs=x_codes[h][:, k, :].bitcast(E4M3),
+                        rhs_scale=x_scale[h][:, k, :],
+                        start=(k == 0),
+                        stop=(k == TG - 1),
+                    )
+                nc.vector.scalar_tensor_tensor(
+                    out=y[g][:, t, hosts], in0=fed[:], scalar=u[:, g, t : t + 1], in1=xt[h][:, g, :, t], op0=MULT, op1=ADD
+                )
+                nc.scalar.copy(
+                    out=y_round[g, h][:, t, :].rearrange("p (s q e) -> p s q e", s=2, e=2),
+                    in_=y[g][:, t, hosts].rearrange("p (q s e) -> p s q e", s=2, e=2),
+                )
+                side()
+
+        def quantize_y(g, h, y_quads, half):
+            cols = slice(256 * half, 256 * (half + 1))
+            nc.vector.quantize_mx(
+                out=y_codes[g, h][:, cols].bitcast(E4M3),
+                scales=y_scale[g, h][:, cols],
+                in_=y_quads[:, cols, :].rearrange("p m e -> p (m e)"),
+            )
+
+        def transpose_y(g, h):
+            y_codes[g, h] = ring.tile([P, K_PASS], U32, tag="y_codes", bufs=6, name="y_codes", align_bytes=64)
+            y_scale[g, h] = ring.tile([P, K_PASS], U8, tag="y_scale", bufs=6, name="y_scale", align_bytes=64)
+            y_quads = ring.tile([P, K_PASS, 4], BF16, tag="y_quads", bufs=2, name="y_quads", align_bytes=64)
+            for half in range(2):
+                turned = psum.tile([P, 4, P], F32, tag="tr", bufs=3, name="turned")
+                for i in range(2):
+                    words = y_round[g, h][:, 2 * half + i, :].bitcast(F32)
+                    for s in range(2):
+                        nc.tensor.transpose(turned[:, 2 * i + s, :], words[:, P * s : P * (s + 1)], ident[:])
+                nc.scalar.copy(
+                    out=y_quads[:, 256 * half : 256 * (half + 1), :].rearrange("p m e -> p (m e)").bitcast(F32).rearrange("p (i m s) -> p i m s", i=2, s=2),
+                    in_=turned[:].rearrange("p (i s) m -> p i m s", s=2),
+                )
+            for half in range(2):
+                queue.append((quantize_y, g, h, y_quads, half))
+
+        def quantize_z(g, c, n, z_quads):
+            cols = slice(P * c, P * (c + n))
+            nc.vector.quantize_mx(
+                out=z_codes[g][:, cols].bitcast(E4M3),
+                scales=z_scale[g][:, cols],
+                in_=z_quads.rearrange("p c m e -> p (c m e)"),
+            )
+
+        def stage_two(g, c):
+            shared = psum.tile([P, 4, P], F32, tag="mm", bufs=5, name="shared")
+            for t in range(4):
+                for h in range(HG):
+                    nc.tensor.matmul_mx(
+                        out=shared[:, t, :],
+                        lhsT=y_codes[g, h][:, P * t : P * (t + 1)].bitcast(E4M3),
+                        lhsT_scale=y_scale[g, h][:, P * t : P * (t + 1)],
+                        rhs=c_codes[:, h, 256 * c : 256 * (c + 1)].bitcast(E2M1),
+                        rhs_scale=c_scale[:, h, P * c : P * (c + 1)],
+                        start=(h == 0),
+                        stop=(h == HG - 1),
+                    )
+            if c % 2 == 0:
+                z_pair[g] = ring.tile([P, 2, P, 4], BF16, tag="z_quads", bufs=3, name="z_quads", align_bytes=64)
+            z_quads = z_pair[g]
+            nc.vector.tensor_tensor(
+                out=z_quads[:, c % 2, :, :],
+                in0=shared[:].rearrange("p t m -> p m t"),
+                in1=y[g][:, :, P * c : P * (c + 1)].rearrange("p t m -> p m t"),
+                op=ADD,
+            )
+            side()
+            if g == TG - 1:
+                queue.append((quantize_z, g, c, 1, z_quads[:, c % 2 : c % 2 + 1, :, :]))
+            elif c % 2 == 1:
+                queue.append((quantize_z, g, c - 1, 2, z_quads[:]))
+
+        def stage_three(c):
+            press = psum.tile([P, MON], F32, tag="mm", bufs=5, name="press")
+            for g in range(TG):
+                nc.tensor.matmul_mx(
+                    out=press[:],
+                    lhsT=z_codes[g][:, P * c : P * (c + 1)].bitcast(E4M3),
+                    lhsT_scale=z_scale[g][:, P * c : P * (c + 1)],
+                    rhs=b_codes[:, g, :].bitcast(E2M1),
+                    rhs_scale=b_scale[:, g, :],
+                    start=(g == 0),
+                    stop=(g == TG - 1),
+                )
+            loss = ring.tile([P, MON], F32, tag="loss", bufs=4, name="loss")
+            growth = ring.tile([P, MON], F32, tag="growth", bufs=3, name="growth")
+            nc.vector.tensor_tensor(out=loss[:], in0=press[:], in1=gates[:, c, :], op=MULT)
+            engine = nc.gpsimd if c < HB - 2 else nc.vector
+            engine.tensor_tensor(out=growth[:], in0=rates[:], in1=loss[:], op=SUB)
+            nc.sync.dma_start(out=out[P * c : P * (c + 1), :], in_=growth[:])
+
+        for k in range(TG):
+            permute_codes(0, k)
+        transpose_x_pair(0, "SSV")
+        for k in range(TG):
+            permute_scales(0, k)
+        for k in range(TG):
+            quantize_x(0, k)
+        transpose_x_pair(1, "SVS")
+        for k in range(TG):
+            quantize_x(1, k)
+        stage_one(0, 0, (0, 1))
+        transpose_x_pair(2, "SSS")
+        queue_permute(1)
+        for i in range(2):
+            side()
+        stage_one(0, 0, (2, 3))
+        transpose_x_pair(3, "SSS")
+        for j in (2, 3):
+            for k in range(TG):
+                queue.append((quantize_x, j, k))
+        for i in range(5):
+            side()
+        stage_one(1, 0)
+        flush()
+        queue_permute(2)
+        stage_one(0, 1)
+        transpose_y(0, 0)
+        stage_one(1, 1, (0, 1))
+        transpose_y(0, 1)
+        stage_one(1, 1, (2, 3))
+        flush()
+        stage_one(2, 0, (0,))
+        for i in range(HB):
+            stage_two(0, i)
+            if i in (1, 3):
+                transpose_y(1, i // 2)
+            if i < 7:
+                stage_one(2, (i + 1) // 4, ((i + 1) % 4,))
+            if i == 5:
+                transpose_y(2, 0)
+        for c in range(2):
+            stage_two(1, c)
+        transpose_y(2, 1)
+        for c in range(2, HB):
+            stage_two(1, c)
+        for c in range(HB):
+            stage_two(2, c)
+            if c >= 3:
+                stage_three(c - 3)
+        flush()
+        for c in range(HB - 3, HB):
+            stage_three(c)

@@ -239,15 +239,16 @@ def tile_microbiome_gated_growth_t2_kernel(
                 z_pair[g] = ring.tile([P, 2, P, 4], BF16, tag="z_quads", bufs=3, name="z_quads", align_bytes=64)
             z_quads = z_pair[g]
             nc.vector.tensor_tensor(
-                out=z_quads[:, c % 2, :, :],
-                in0=shared[:].rearrange("p t m -> p m t"),
-                in1=y[g][:, :, P * c : P * (c + 1)].rearrange("p t m -> p m t"),
+                out=z_quads[:, c % 2, :, :].rearrange("p (m i) t -> p m t i", i=4),
+                in0=shared[:].rearrange("p t (m i) -> p m t i", i=4),
+                in1=y[g][:, :, P * c : P * (c + 1)].rearrange("p t (m i) -> p m t i", i=4),
                 op=ADD,
             )
-            side()
-            if g == TG - 1:
+            if g < TG - 1:
+                side()
+            else:
                 queue.append((quantize_z, g, c, 1, z_quads[:, c % 2 : c % 2 + 1, :, :]))
-            elif c % 2 == 1:
+            if g < TG - 1 and c % 2 == 1:
                 queue.append((quantize_z, g, c - 1, 2, z_quads[:]))
 
         def stage_three(c):
@@ -262,8 +263,8 @@ def tile_microbiome_gated_growth_t2_kernel(
                     start=(g == 0),
                     stop=(g == TG - 1),
                 )
-            loss = ring.tile([P, MON], F32, tag="loss", bufs=4, name="loss")
-            growth = ring.tile([P, MON], F32, tag="growth", bufs=3, name="growth")
+            loss = ring.tile([P, MON], F32, tag="loss", bufs=3, name="loss")
+            growth = ring.tile([P, MON], F32, tag="growth", bufs=4, name="growth")
             nc.vector.tensor_tensor(out=loss[:], in0=press[:], in1=gates[:, c, :], op=MULT)
             engine = nc.gpsimd if c < HB - 2 else nc.vector
             engine.tensor_tensor(out=growth[:], in0=rates[:], in1=loss[:], op=SUB)
@@ -318,6 +319,7 @@ def tile_microbiome_gated_growth_t2_kernel(
             stage_two(2, c)
             if c >= 3:
                 stage_three(c - 3)
+            side()
         flush()
         for c in range(HB - 3, HB):
             stage_three(c)

@@ -18,6 +18,8 @@ MULT = mybir.AluOpType.mult
 SUB = mybir.AluOpType.subtract
 
 P = 128
+LAGS = (1, 2, 1, 2, 1, 1, 0)
+STT, ROUND, QX, QY, ZADD, QZ, GATE = LAGS
 K_PASS = 512
 TG = TAXA // K_PASS
 HG = HOSTS // K_PASS
@@ -34,12 +36,14 @@ def tile_microbiome_gated_growth_t2_kernel(
         psum = ctx.enter_context(tc.psum_pool(name="psum", bufs=4))
         ctx.enter_context(tc.manual_schedule())
 
-        a_scale_in = keep.tile([P, TG, TAXA], U8, align_bytes=64)
+        a_scale_in = [keep.tile([P, TG, K_PASS], U8, name=f"a_scale_in{g}", align_bytes=64) for g in range(TG)]
         c_scale = keep.tile([P, HG, HOSTS], U8, align_bytes=64)
         b_scale = keep.tile([P, TG, MON], U8, align_bytes=64)
         ident = keep.tile([P, P], F32)
-        nc.vector.memset(a_scale_in[:].rearrange("p k n -> p (k n)").bitcast(I32), 0)
+        nc.vector.memset(a_scale_in[0][:].rearrange("p k n -> p (k n)").bitcast(I32), 0)
         make_identity(nc, ident[:])
+        for g in range(1, TG):
+            nc.gpsimd.memset(a_scale_in[g][:].rearrange("p k n -> p (k n)").bitcast(I32), 0)
         nc.gpsimd.memset(c_scale[:].rearrange("p k n -> p (k n)").bitcast(I32), 0)
         nc.gpsimd.memset(b_scale[:].rearrange("p k n -> p (k n)").bitcast(I32), 0)
 
@@ -68,17 +72,20 @@ def tile_microbiome_gated_growth_t2_kernel(
                     in_=rows[:, 4 * q : 4 * q + 4, :].rearrange("k q n -> q k n").bitcast(I32),
                 )
 
-        load_x(0)
+        def load_a_scales(g):
+            load_scales(a_scale_in[g], feed_scales[:, :, K_PASS * g : K_PASS * (g + 1)])
+
         load_a(0)
-        load_x(1)
-        load_scales(a_scale_in, feed_scales)
-        for i in range(2, 6):
+        load_a_scales(0)
+        for i in range(4):
             load_x(i)
         nc.sync.dma_start(out=u[:], in_=uptake.rearrange("(g p t) -> p g t", g=TG, t=4))
         load_a(1)
-        load_x(6)
-        load_x(7)
+        load_a_scales(1)
+        for i in range(4, HB):
+            load_x(i)
         load_a(2)
+        load_a_scales(2)
         nc.sync.dma_start(out=c_codes[:].bitcast(I32), in_=share_words.rearrange("k p b -> p k b").bitcast(I32))
         load_scales(c_scale, share_scales)
         nc.sync.dma_start(out=b_codes[:].bitcast(I32), in_=inhib_words.rearrange("k p b -> p k b").bitcast(I32))
@@ -96,36 +103,37 @@ def tile_microbiome_gated_growth_t2_kernel(
         z_scale = [keep.tile([P, HOSTS], U8, name=f"z_scale{g}", align_bytes=64) for g in range(TG)]
         y_codes, y_scale, y_round = {}, {}, {}
         z_pair = {}
+        x_words = {}
 
-        queue = []
+        work = [[] for i in range(200)]
+        beat = [0]
 
-        def side():
-            if queue:
-                piece = queue[0]
-                queue.remove(piece)
+        def after(lag, *piece):
+            work[beat[0] + lag].append(piece)
+
+        def run(block, *args):
+            block(*args)
+            for piece in work[beat[0]]:
                 piece[0](*piece[1:])
+            beat[0] += 1
 
-        def flush():
-            while queue:
-                side()
-
-        def permute_codes(g, k):
+        def permute(g, t):
             nc.vector.tensor_copy(
-                out=a_codes[g][:, k, :].rearrange("p (t m b) -> p t m b", t=4, b=2),
-                in_=a_in[g][:, k, :].rearrange("p (m t b) -> p t m b", t=4, b=2),
+                out=a_codes[g][:, :, 256 * t : 256 * (t + 1)].rearrange("p k (m b) -> p k m b", b=2),
+                in_=a_in[g][:].rearrange("p k (m t b) -> p k t m b", t=4, b=2)[:, :, t, :, :],
+            )
+            nc.vector.tensor_copy(
+                out=a_scale[g][:, :, P * t : P * (t + 1)],
+                in_=a_scale_in[g][:].rearrange("p k (m t) -> p k t m", t=4)[:, :, t, :],
             )
 
-        def permute_scales(g, k):
-            nc.vector.tensor_copy(
-                out=a_scale[g][:, k, :].rearrange("p (t m) -> p t m", t=4),
-                in_=a_scale_in[:, k, K_PASS * g : K_PASS * (g + 1)].rearrange("p (m t) -> p t m", t=4),
-            )
-
-        def queue_permute(g):
-            for k in range(TG):
-                queue.append((permute_codes, g, k))
-            for k in range(TG):
-                queue.append((permute_scales, g, k))
+        def reorder_x(i):
+            x_words[i] = ring.tile([P, TG, 2, P, 2], BF16, tag="x_words", bufs=3, name="x_words", align_bytes=64)
+            for s in range(2):
+                nc.scalar.copy(
+                    out=x_words[i][:].rearrange("p k s q e -> p (k s q e)").bitcast(F32).rearrange("p (k s q) -> p s k q", k=TG, s=2)[:, s, :, :],
+                    in_=x_in[i][:].bitcast(F32).rearrange("p (k q s) -> p s k q", k=TG, s=2)[:, s, :, :],
+                )
 
         def copy_out(engine, out, in_):
             if engine == "S":
@@ -133,61 +141,84 @@ def tile_microbiome_gated_growth_t2_kernel(
             else:
                 nc.vector.tensor_copy(out=out, in_=in_)
 
-        def transpose_x_pair(j, engines):
-            h, base = j // 2, 256 * (j % 2)
-            last = psum.tile([P, 4, P], F32, tag="tr", bufs=3, name="tr_last")
-            for i in range(2):
-                words = x_in[2 * j + i][:].bitcast(F32)
-                first = psum.tile([P, 4, P], F32, tag="tr", bufs=3, name="tr_first")
-                for k in range(TG):
+        def transpose_x(i, engines="SS"):
+            h, cols = i // 4, slice(P * (i % 4), P * (i % 4 + 1))
+            if i in x_words:
+                words = x_words[i][:].rearrange("p k s q e -> p (k s q e)").bitcast(F32)
+            else:
+                words = x_in[i][:].bitcast(F32)
+            for k in range(TG):
+                after(QX, quantize_x, i, 1, k)
+            for part, ks in enumerate(((0, 1), (2,))):
+                turned = psum.tile([P, 4, P], F32, tag="tr", bufs=3, name="turned")
+                for j, k in enumerate(ks):
                     for s in range(2):
-                        dst = first[:, 2 * k + s, :] if k < 2 else last[:, 2 * i + s, :]
-                        nc.tensor.transpose(dst, words[:, 256 * k + s : 256 * (k + 1) : 2], ident[:])
-                cols = slice(base + P * i, base + P * (i + 1))
+                        if i in x_words:
+                            cut = words[:, 256 * k + P * s : 256 * k + P * (s + 1)]
+                        else:
+                            cut = words[:, 256 * k + s : 256 * (k + 1) : 2]
+                        nc.tensor.transpose(turned[:, 2 * j + s, :], cut, ident[:])
                 copy_out(
-                    engines[i],
-                    out=xt[h][:, 0:2, cols, :].rearrange("p k m e -> p k (m e)").bitcast(F32).rearrange("p k (m s) -> p k m s", s=2),
-                    in_=first[:].rearrange("p (k s) m -> p k m s", s=2),
+                    engines[part],
+                    out=xt[h][:, ks[0] : ks[-1] + 1, cols, :].rearrange("p k m e -> p k (m e)").bitcast(F32).rearrange("p k (m s) -> p k m s", s=2),
+                    in_=turned[:, 0 : 2 * len(ks), :].rearrange("p (k s) m -> p k m s", s=2),
                 )
-            copy_out(
-                engines[2],
-                out=xt[h][:, 2, base : base + 256, :].rearrange("p m e -> p (m e)").bitcast(F32).rearrange("p (i m s) -> p i m s", i=2, s=2),
-                in_=last[:].rearrange("p (i s) m -> p i m s", s=2),
-            )
 
-        def quantize_x(j, k):
-            h, base = j // 2, 256 * (j % 2)
-            cols = slice(base, base + 256)
+        def quantize_x(i, n, k):
+            h, cols = i // 4, slice(P * (i % 4), P * (i % 4 + n))
             nc.vector.quantize_mx(
                 out=x_codes[h][:, k, cols].bitcast(E4M3),
                 scales=x_scale[h][:, k, cols],
                 in_=xt[h][:, k, cols, :].rearrange("p m e -> p (m e)"),
             )
 
-        def stage_one(g, h, tiles=range(4)):
-            if 0 in tiles:
-                y_round[g, h] = ring.tile([P, 4, K_PASS], BF16, tag="y_round", bufs=3, name="y_round", align_bytes=64)
+        first_fed = {}
+
+        def add_uptake(g, h, t, fed):
             hosts = slice(K_PASS * h, K_PASS * (h + 1))
-            for t in tiles:
-                fed = psum.tile([P, K_PASS], F32, tag="mm", bufs=5, name="fed")
-                for k in range(TG):
-                    nc.tensor.matmul_mx(
-                        out=fed[:],
-                        lhsT=a_codes[g][:, k, 256 * t : 256 * (t + 1)].bitcast(E2M1),
-                        lhsT_scale=a_scale[g][:, k, P * t : P * (t + 1)],
-                        rhs=x_codes[h][:, k, :].bitcast(E4M3),
-                        rhs_scale=x_scale[h][:, k, :],
-                        start=(k == 0),
-                        stop=(k == TG - 1),
-                    )
-                nc.vector.scalar_tensor_tensor(
-                    out=y[g][:, t, hosts], in0=fed[:], scalar=u[:, g, t : t + 1], in1=xt[h][:, g, :, t], op0=MULT, op1=ADD
+            nc.vector.scalar_tensor_tensor(
+                out=y[g][:, t, hosts], in0=fed[:], scalar=u[:, g, t : t + 1], in1=xt[h][:, g, :, t], op0=MULT, op1=ADD
+            )
+            after(ROUND, round_y, g, h, t)
+
+        def round_y(g, h, t):
+            hosts = slice(K_PASS * h, K_PASS * (h + 1))
+            nc.scalar.copy(
+                out=y_round[g, h][:, t, :].rearrange("p (s q e) -> p s q e", s=2, e=2),
+                in_=y[g][:, t, hosts].rearrange("p (q s e) -> p s q e", s=2, e=2),
+            )
+
+        def feed(g, h, t, fed, hosts):
+            for k in range(TG):
+                nc.tensor.matmul_mx(
+                    out=fed[:, hosts],
+                    lhsT=a_codes[g][:, k, 256 * t : 256 * (t + 1)].bitcast(E2M1),
+                    lhsT_scale=a_scale[g][:, k, P * t : P * (t + 1)],
+                    rhs=x_codes[h][:, k, hosts].bitcast(E4M3),
+                    rhs_scale=x_scale[h][:, k, hosts],
+                    start=(k == 0),
+                    stop=(k == TG - 1),
                 )
-                nc.scalar.copy(
-                    out=y_round[g, h][:, t, :].rearrange("p (s q e) -> p s q e", s=2, e=2),
-                    in_=y[g][:, t, hosts].rearrange("p (q s e) -> p s q e", s=2, e=2),
-                )
-                side()
+
+        def new_round(g, h):
+            y_round[g, h] = ring.tile([P, 4, K_PASS], BF16, tag="y_round", bufs=3, name="y_round", align_bytes=64)
+
+        def first_stage_one(i):
+            if i == 0:
+                new_round(0, 0)
+            for t in range(4):
+                if i == 0:
+                    first_fed[t] = psum.tile([P, K_PASS], F32, tag="mm", bufs=5, name="fed")
+                feed(0, 0, t, first_fed[t], slice(P * i, P * (i + 1)))
+                if i == 3:
+                    after(STT + t // 2, add_uptake, 0, 0, t, first_fed[t])
+
+        def stage_one(g, h, t):
+            if t == 0:
+                new_round(g, h)
+            fed = psum.tile([P, K_PASS], F32, tag="mm", bufs=5, name="fed")
+            feed(g, h, t, fed, slice(0, K_PASS))
+            after(STT, add_uptake, g, h, t, fed)
 
         def quantize_y(g, h, y_quads, half):
             cols = slice(256 * half, 256 * (half + 1))
@@ -212,14 +243,14 @@ def tile_microbiome_gated_growth_t2_kernel(
                     in_=turned[:].rearrange("p (i s) m -> p i m s", s=2),
                 )
             for half in range(2):
-                queue.append((quantize_y, g, h, y_quads, half))
+                after(QY + half, quantize_y, g, h, y_quads, half)
 
         def quantize_z(g, c, n, z_quads):
             cols = slice(P * c, P * (c + n))
             nc.vector.quantize_mx(
                 out=z_codes[g][:, cols].bitcast(E4M3),
                 scales=z_scale[g][:, cols],
-                in_=z_quads.rearrange("p c m e -> p (c m e)"),
+                in_=z_quads[:, 0:n, :, :].rearrange("p c m e -> p (c m e)"),
             )
 
         def stage_two(g, c):
@@ -235,21 +266,21 @@ def tile_microbiome_gated_growth_t2_kernel(
                         start=(h == 0),
                         stop=(h == HG - 1),
                     )
+            after(ZADD, add_y, g, c, shared)
+
+        def add_y(g, c, shared):
             if c % 2 == 0:
                 z_pair[g] = ring.tile([P, 2, P, 4], BF16, tag="z_quads", bufs=3, name="z_quads", align_bytes=64)
-            z_quads = z_pair[g]
             nc.vector.tensor_tensor(
-                out=z_quads[:, c % 2, :, :].rearrange("p (m i) t -> p m t i", i=4),
+                out=z_pair[g][:, c % 2, :, :].rearrange("p (m i) t -> p m t i", i=4),
                 in0=shared[:].rearrange("p t (m i) -> p m t i", i=4),
                 in1=y[g][:, :, P * c : P * (c + 1)].rearrange("p t (m i) -> p m t i", i=4),
                 op=ADD,
             )
-            if g < TG - 1:
-                side()
-            else:
-                queue.append((quantize_z, g, c, 1, z_quads[:, c % 2 : c % 2 + 1, :, :]))
-            if g < TG - 1 and c % 2 == 1:
-                queue.append((quantize_z, g, c - 1, 2, z_quads[:]))
+            if g == TG - 1:
+                after(QZ, quantize_z, g, c, 1, z_pair[g][:, c % 2 : c % 2 + 1, :, :])
+            elif c % 2 == 1:
+                after(QZ, quantize_z, g, c - 1, 2, z_pair[g])
 
         def stage_three(c):
             press = psum.tile([P, MON], F32, tag="mm", bufs=5, name="press")
@@ -263,63 +294,108 @@ def tile_microbiome_gated_growth_t2_kernel(
                     start=(g == 0),
                     stop=(g == TG - 1),
                 )
-            loss = ring.tile([P, MON], F32, tag="loss", bufs=3, name="loss")
-            growth = ring.tile([P, MON], F32, tag="growth", bufs=4, name="growth")
-            nc.vector.tensor_tensor(out=loss[:], in0=press[:], in1=gates[:, c, :], op=MULT)
-            engine = nc.gpsimd if c < HB - 2 else nc.vector
-            engine.tensor_tensor(out=growth[:], in0=rates[:], in1=loss[:], op=SUB)
-            nc.sync.dma_start(out=out[P * c : P * (c + 1), :], in_=growth[:])
+            after(GATE, apply_gate, c, press)
 
-        for k in range(TG):
-            permute_codes(0, k)
-        transpose_x_pair(0, "SSV")
-        for k in range(TG):
-            permute_scales(0, k)
-        for k in range(TG):
-            quantize_x(0, k)
-        transpose_x_pair(1, "SVS")
-        for k in range(TG):
-            quantize_x(1, k)
-        stage_one(0, 0, (0, 1))
-        transpose_x_pair(2, "SSS")
-        queue_permute(1)
-        for i in range(2):
-            side()
-        stage_one(0, 0, (2, 3))
-        transpose_x_pair(3, "SSS")
-        for j in (2, 3):
-            for k in range(TG):
-                queue.append((quantize_x, j, k))
-        for i in range(5):
-            side()
-        stage_one(1, 0)
-        flush()
-        queue_permute(2)
-        stage_one(0, 1)
-        transpose_y(0, 0)
-        stage_one(1, 1, (0, 1))
-        transpose_y(0, 1)
-        stage_one(1, 1, (2, 3))
-        flush()
-        stage_one(2, 0, (0,))
-        for i in range(HB):
-            stage_two(0, i)
-            if i in (1, 3):
-                transpose_y(1, i // 2)
-            if i < 7:
-                stage_one(2, (i + 1) // 4, ((i + 1) % 4,))
-            if i == 5:
-                transpose_y(2, 0)
-        for c in range(2):
-            stage_two(1, c)
-        transpose_y(2, 1)
-        for c in range(2, HB):
-            stage_two(1, c)
-        for c in range(HB):
-            stage_two(2, c)
-            if c >= 3:
-                stage_three(c - 3)
-            side()
-        flush()
-        for c in range(HB - 3, HB):
-            stage_three(c)
+        def apply_gate(c, press):
+            loss = ring.tile([P, MON], F32, tag="loss", bufs=3, name="loss")
+            growth = ring.tile([P, MON], F32, tag="growth", bufs=6, name="growth")
+            parts = 1 if c < HB - 1 else 2
+            engine = nc.gpsimd if c < 4 or c % 2 == 0 else nc.vector
+            spans = [slice(MON // parts * j, MON // parts * (j + 1)) for j in range(parts)]
+            for cols in spans:
+                nc.vector.tensor_tensor(out=loss[:, cols], in0=press[:, cols], in1=gates[:, c, cols], op=MULT)
+            for cols in spans:
+                engine.tensor_tensor(out=growth[:, cols], in0=rates[:, cols], in1=loss[:, cols], op=SUB)
+                nc.sync.dma_start(out=out[P * c : P * (c + 1), cols], in_=growth[:, cols])
+
+        for block in (
+            (permute, 0, 0),
+            (permute, 0, 1),
+            (transpose_x, 0),
+            (permute, 0, 2),
+            (transpose_x, 1),
+            (permute, 0, 3),
+            (permute, 1, 0),
+            (transpose_x, 2),
+            (transpose_x, 3),
+            (first_stage_one, 0),
+            (first_stage_one, 1),
+            (permute, 1, 1),
+            (reorder_x, 4),
+            (permute, 1, 2),
+            (permute, 1, 3),
+            (reorder_x, 5),
+            (reorder_x, 6),
+            (first_stage_one, 2),
+            (transpose_x, 4),
+            (stage_one, 1, 0, 0),
+            (transpose_x, 5),
+            (permute, 2, 0),
+            (stage_one, 1, 0, 1),
+            (reorder_x, 7),
+            (stage_one, 1, 0, 2),
+            (transpose_x, 6),
+            (stage_one, 1, 0, 3),
+            (transpose_x, 7),
+            (stage_one, 2, 0, 0),
+            (first_stage_one, 3),
+            (stage_one, 0, 1, 0),
+            (stage_one, 0, 1, 1),
+            (stage_one, 0, 1, 2),
+            (stage_one, 1, 1, 0),
+            (permute, 2, 1),
+            (stage_one, 0, 1, 3),
+            (transpose_y, 1, 0),
+            (stage_one, 2, 1, 0),
+            (stage_one, 1, 1, 1),
+            (transpose_y, 0, 0),
+            (stage_one, 1, 1, 2),
+            (permute, 2, 2),
+            (transpose_y, 0, 1),
+            (stage_one, 1, 1, 3),
+            (permute, 2, 3),
+            (stage_one, 2, 0, 1),
+            (stage_one, 2, 1, 1),
+            (stage_one, 2, 1, 2),
+            (stage_two, 0, 0),
+            (transpose_y, 1, 1),
+            (stage_two, 0, 1),
+            (stage_one, 2, 0, 2),
+            (stage_two, 0, 2),
+            (stage_one, 2, 0, 3),
+            (stage_two, 1, 0),
+            (stage_one, 2, 1, 3),
+            (stage_two, 1, 1),
+            (stage_two, 1, 2),
+            (stage_two, 1, 3),
+            (stage_two, 0, 3),
+            (stage_two, 0, 4),
+            (transpose_y, 2, 0),
+            (stage_two, 0, 5),
+            (transpose_y, 2, 1),
+            (stage_two, 1, 4),
+            (stage_two, 0, 6),
+            (stage_two, 1, 5),
+            (stage_two, 0, 7),
+            (stage_two, 2, 0),
+            (stage_two, 2, 1),
+            (stage_two, 1, 6),
+            (stage_two, 2, 2),
+            (stage_two, 2, 3),
+            (stage_two, 2, 4),
+            (stage_three, 0),
+            (stage_two, 2, 5),
+            (stage_two, 2, 6),
+            (stage_three, 1),
+            (stage_two, 1, 7),
+            (stage_three, 2),
+            (stage_three, 3),
+            (stage_two, 2, 7),
+            (stage_three, 4),
+            (stage_three, 5),
+            (stage_three, 6),
+            (stage_three, 7),
+        ):
+            run(*block)
+        for i in range(8):
+            run(len, ())

@@ -18,8 +18,11 @@ MULT = mybir.AluOpType.mult
 SUB = mybir.AluOpType.subtract
 
 P = 128
-LAGS = (1, 2, 1, 2, 1, 1, 0)
-STT, ROUND, QX, QY, ZADD, QZ, GATE = LAGS
+LAGS = (1, 1, 3, 1, 1, 0, 7)
+LOADS = (("u", 0), ("x", 0), ("x", 1), ("x", 2), ("s", 1), ("a", 0), ("x", 3), ("x", 4), ("s", 0), ("x", 5), ("x", 6), ("x", 7), ("a", 1), ("a", 2), ("s", 2))
+STT, ROUND, QY, ZADD, QZ, GATE, GROUND = LAGS
+COPY = mybir.ActivationFunctionType.Copy
+ZN = (4, 4, 2)
 K_PASS = 512
 TG = TAXA // K_PASS
 HG = HOSTS // K_PASS
@@ -52,6 +55,7 @@ def tile_microbiome_gated_growth_t2_kernel(
         c_codes = keep.tile([P, HG, 2 * HOSTS], U8, align_bytes=64)
         b_codes = keep.tile([P, TG, 2 * MON], U8, align_bytes=64)
         u = keep.tile([P, TG, 4], BF16, align_bytes=64)
+        u_wide = keep.tile([P, TG, 4], F32, align_bytes=64)
         gates = keep.tile([P, HB, MON], BF16, align_bytes=64)
         rates = keep.tile([P, MON], BF16, align_bytes=64)
 
@@ -75,17 +79,11 @@ def tile_microbiome_gated_growth_t2_kernel(
         def load_a_scales(g):
             load_scales(a_scale_in[g], feed_scales[:, :, K_PASS * g : K_PASS * (g + 1)])
 
-        load_a(0)
-        load_a_scales(0)
-        for i in range(4):
-            load_x(i)
-        nc.sync.dma_start(out=u[:], in_=uptake.rearrange("(g p t) -> p g t", g=TG, t=4))
-        load_a(1)
-        load_a_scales(1)
-        for i in range(4, HB):
-            load_x(i)
-        load_a(2)
-        load_a_scales(2)
+        def load_u():
+            nc.sync.dma_start(out=u[:], in_=uptake.rearrange("(g p t) -> p g t", g=TG, t=4))
+
+        for kind, i in LOADS:
+            {"x": load_x, "a": load_a, "s": load_a_scales, "u": lambda i: load_u()}[kind](i)
         nc.sync.dma_start(out=c_codes[:].bitcast(I32), in_=share_words.rearrange("k p b -> p k b").bitcast(I32))
         load_scales(c_scale, share_scales)
         nc.sync.dma_start(out=b_codes[:].bitcast(I32), in_=inhib_words.rearrange("k p b -> p k b").bitcast(I32))
@@ -96,8 +94,8 @@ def tile_microbiome_gated_growth_t2_kernel(
         xt = [keep.tile([P, TG, K_PASS, 4], BF16, name=f"xt{h}", align_bytes=64) for h in range(HG)]
         x_codes = [keep.tile([P, TG, K_PASS], U32, name=f"x_codes{h}", align_bytes=64) for h in range(HG)]
         x_scale = [keep.tile([P, TG, K_PASS], U8, name=f"x_scale{h}", align_bytes=64) for h in range(HG)]
-        a_codes = [keep.tile([P, TG, 2 * K_PASS], U8, name=f"a_codes{g}", align_bytes=64) for g in range(TG)]
-        a_scale = [keep.tile([P, TG, K_PASS], U8, name=f"a_scale{g}", align_bytes=64) for g in range(TG)]
+        a_codes = [keep.tile([P, 4, TG, 2 * P], U8, name=f"a_codes{g}", align_bytes=64) for g in range(TG)]
+        a_scale = [keep.tile([P, 4, TG, P], U8, name=f"a_scale{g}", align_bytes=64) for g in range(TG)]
         y = [keep.tile([P, 4, HOSTS], F32, name=f"y{g}", align_bytes=64) for g in range(TG)]
         z_codes = [keep.tile([P, HOSTS], U32, name=f"z_codes{g}", align_bytes=64) for g in range(TG)]
         z_scale = [keep.tile([P, HOSTS], U8, name=f"z_scale{g}", align_bytes=64) for g in range(TG)]
@@ -113,66 +111,54 @@ def tile_microbiome_gated_growth_t2_kernel(
 
         def run(block, *args):
             block(*args)
+            if block in (permute, quantize_x, reorder_x, widen_uptake):
+                return
             for piece in work[beat[0]]:
                 piece[0](*piece[1:])
             beat[0] += 1
 
-        def permute(g, t):
+        def permute(g, t, n):
             nc.vector.tensor_copy(
-                out=a_codes[g][:, :, 256 * t : 256 * (t + 1)].rearrange("p k (m b) -> p k m b", b=2),
-                in_=a_in[g][:].rearrange("p k (m t b) -> p k t m b", t=4, b=2)[:, :, t, :, :],
+                out=a_codes[g][:, t : t + n, :, :].rearrange("p t k (m b) -> p t (k m) b", b=2),
+                in_=a_in[g][:].rearrange("p k (m t b) -> p t (k m) b", t=4, b=2)[:, t : t + n, :, :],
             )
             nc.vector.tensor_copy(
-                out=a_scale[g][:, :, P * t : P * (t + 1)],
-                in_=a_scale_in[g][:].rearrange("p k (m t) -> p k t m", t=4)[:, :, t, :],
+                out=a_scale[g][:, t : t + n, :, :].rearrange("p t k m -> p t (k m)"),
+                in_=a_scale_in[g][:].rearrange("p k (m t) -> p t (k m)", t=4)[:, t : t + n, :],
             )
 
         def reorder_x(i):
-            x_words[i] = ring.tile([P, TG, 2, P, 2], BF16, tag="x_words", bufs=3, name="x_words", align_bytes=64)
-            for s in range(2):
-                nc.scalar.copy(
-                    out=x_words[i][:].rearrange("p k s q e -> p (k s q e)").bitcast(F32).rearrange("p (k s q) -> p s k q", k=TG, s=2)[:, s, :, :],
-                    in_=x_in[i][:].bitcast(F32).rearrange("p (k q s) -> p s k q", k=TG, s=2)[:, s, :, :],
-                )
+            x_words[i] = ring.tile([P, 2, TG, P], F32, tag="x_words", bufs=1, name="x_words", align_bytes=64)
+            nc.scalar.copy(
+                out=x_words[i][:].rearrange("p s k q -> p s (k q)"),
+                in_=x_in[i][:].bitcast(F32).rearrange("p (w s) -> p s w", s=2),
+            )
 
-        def copy_out(engine, out, in_):
-            if engine == "S":
-                nc.scalar.copy(out=out, in_=in_)
-            else:
-                nc.vector.tensor_copy(out=out, in_=in_)
+        def transpose_x_words(i):
+            transpose_x(i, True)
 
-        def transpose_x(i, engines="SS"):
+        def transpose_x(i, reordered=False):
             h, cols = i // 4, slice(P * (i % 4), P * (i % 4 + 1))
-            if i in x_words:
-                words = x_words[i][:].rearrange("p k s q e -> p (k s q e)").bitcast(F32)
-            else:
-                words = x_in[i][:].bitcast(F32)
-            for k in range(TG):
-                after(QX, quantize_x, i, 1, k)
-            for part, ks in enumerate(((0, 1), (2,))):
-                turned = psum.tile([P, 4, P], F32, tag="tr", bufs=3, name="turned")
+            words = x_in[i][:].bitcast(F32)
+            for ks in ((0, 1), (2,)):
+                turned = psum.tile([P, 4, P], F32, tag="tr", bufs=4, name="turned")
                 for j, k in enumerate(ks):
                     for s in range(2):
-                        if i in x_words:
-                            cut = words[:, 256 * k + P * s : 256 * k + P * (s + 1)]
-                        else:
-                            cut = words[:, 256 * k + s : 256 * (k + 1) : 2]
-                        nc.tensor.transpose(turned[:, 2 * j + s, :], cut, ident[:])
-                copy_out(
-                    engines[part],
+                        nc.tensor.transpose(turned[:, 2 * j + s, :], x_words[i][:, s, k, :] if reordered else words[:, 256 * k + s : 256 * (k + 1) : 2], ident[:])
+                nc.scalar.copy(
                     out=xt[h][:, ks[0] : ks[-1] + 1, cols, :].rearrange("p k m e -> p k (m e)").bitcast(F32).rearrange("p k (m s) -> p k m s", s=2),
                     in_=turned[:, 0 : 2 * len(ks), :].rearrange("p (k s) m -> p k m s", s=2),
                 )
 
-        def quantize_x(i, n, k):
-            h, cols = i // 4, slice(P * (i % 4), P * (i % 4 + n))
+        def quantize_x(h, k, n, c0, cn):
+            cols = slice(P * c0, P * (c0 + cn))
+            codes, scale, values = x_codes[h][:, k : k + n, cols], x_scale[h][:, k : k + n, cols], xt[h][:, k : k + n, cols, :]
             nc.vector.quantize_mx(
-                out=x_codes[h][:, k, cols].bitcast(E4M3),
-                scales=x_scale[h][:, k, cols],
-                in_=xt[h][:, k, cols, :].rearrange("p m e -> p (m e)"),
+                out=codes.rearrange("p k m -> p (k m)").bitcast(E4M3),
+                scales=scale.rearrange("p k m -> p (k m)"),
+                in_=values.rearrange("p k m e -> p (k m e)"),
             )
 
-        first_fed = {}
 
         def add_uptake(g, h, t, fed):
             hosts = slice(K_PASS * h, K_PASS * (h + 1))
@@ -181,6 +167,16 @@ def tile_microbiome_gated_growth_t2_kernel(
             )
             after(ROUND, round_y, g, h, t)
 
+        def scale_fed(g, h, t, fed):
+            hosts = slice(K_PASS * h, K_PASS * (h + 1))
+            scaled = ring.tile([P, K_PASS], F32, tag="loss", bufs=3, name="scaled", align_bytes=64)
+            nc.scalar.activation(out=scaled[:], in_=fed[:], func=COPY, scale=u_wide[:, g, t : t + 1])
+            nc.gpsimd.tensor_tensor(out=y[g][:, t, hosts], in0=scaled[:], in1=xt[h][:, g, :, t], op=ADD)
+            after(GROUND, round_y, g, h, t)
+
+        def widen_uptake():
+            nc.vector.tensor_copy(out=u_wide[:], in_=u[:])
+
         def round_y(g, h, t):
             hosts = slice(K_PASS * h, K_PASS * (h + 1))
             nc.scalar.copy(
@@ -188,44 +184,36 @@ def tile_microbiome_gated_growth_t2_kernel(
                 in_=y[g][:, t, hosts].rearrange("p (q s e) -> p s q e", s=2, e=2),
             )
 
-        def feed(g, h, t, fed, hosts):
+        def feed(g, h, t, fed):
             for k in range(TG):
                 nc.tensor.matmul_mx(
-                    out=fed[:, hosts],
-                    lhsT=a_codes[g][:, k, 256 * t : 256 * (t + 1)].bitcast(E2M1),
-                    lhsT_scale=a_scale[g][:, k, P * t : P * (t + 1)],
-                    rhs=x_codes[h][:, k, hosts].bitcast(E4M3),
-                    rhs_scale=x_scale[h][:, k, hosts],
+                    out=fed[:],
+                    lhsT=a_codes[g][:, t, k, :].bitcast(E2M1),
+                    lhsT_scale=a_scale[g][:, t, k, :],
+                    rhs=x_codes[h][:, k, :].bitcast(E4M3),
+                    rhs_scale=x_scale[h][:, k, :],
                     start=(k == 0),
                     stop=(k == TG - 1),
                 )
 
         def new_round(g, h):
-            y_round[g, h] = ring.tile([P, 4, K_PASS], BF16, tag="y_round", bufs=3, name="y_round", align_bytes=64)
+            y_round[g, h] = ring.tile([P, 4, K_PASS], BF16, tag="y_round", bufs=4, name="y_round", align_bytes=64)
 
-        def first_stage_one(i):
-            if i == 0:
-                new_round(0, 0)
-            for t in range(4):
-                if i == 0:
-                    first_fed[t] = psum.tile([P, K_PASS], F32, tag="mm", bufs=5, name="fed")
-                feed(0, 0, t, first_fed[t], slice(P * i, P * (i + 1)))
-                if i == 3:
-                    after(STT + t // 2, add_uptake, 0, 0, t, first_fed[t])
+        def stage_one_aside(g, h, t):
+            stage_one(g, h, t, True)
 
-        def stage_one(g, h, t):
+        def stage_one(g, h, t, aside=False):
             if t == 0:
                 new_round(g, h)
-            fed = psum.tile([P, K_PASS], F32, tag="mm", bufs=5, name="fed")
-            feed(g, h, t, fed, slice(0, K_PASS))
-            after(STT, add_uptake, g, h, t, fed)
+            fed = psum.tile([P, K_PASS], F32, tag="mm", bufs=4, name="fed")
+            feed(g, h, t, fed)
+            after(STT, scale_fed if aside else add_uptake, g, h, t, fed)
 
-        def quantize_y(g, h, y_quads, half):
-            cols = slice(256 * half, 256 * (half + 1))
+        def quantize_y(g, h, y_quads):
             nc.vector.quantize_mx(
-                out=y_codes[g, h][:, cols].bitcast(E4M3),
-                scales=y_scale[g, h][:, cols],
-                in_=y_quads[:, cols, :].rearrange("p m e -> p (m e)"),
+                out=y_codes[g, h][:].bitcast(E4M3),
+                scales=y_scale[g, h][:],
+                in_=y_quads[:].rearrange("p m e -> p (m e)"),
             )
 
         def transpose_y(g, h):
@@ -233,7 +221,7 @@ def tile_microbiome_gated_growth_t2_kernel(
             y_scale[g, h] = ring.tile([P, K_PASS], U8, tag="y_scale", bufs=6, name="y_scale", align_bytes=64)
             y_quads = ring.tile([P, K_PASS, 4], BF16, tag="y_quads", bufs=2, name="y_quads", align_bytes=64)
             for half in range(2):
-                turned = psum.tile([P, 4, P], F32, tag="tr", bufs=3, name="turned")
+                turned = psum.tile([P, 4, P], F32, tag="tr", bufs=4, name="turned")
                 for i in range(2):
                     words = y_round[g, h][:, 2 * half + i, :].bitcast(F32)
                     for s in range(2):
@@ -242,8 +230,7 @@ def tile_microbiome_gated_growth_t2_kernel(
                     out=y_quads[:, 256 * half : 256 * (half + 1), :].rearrange("p m e -> p (m e)").bitcast(F32).rearrange("p (i m s) -> p i m s", i=2, s=2),
                     in_=turned[:].rearrange("p (i s) m -> p i m s", s=2),
                 )
-            for half in range(2):
-                after(QY + half, quantize_y, g, h, y_quads, half)
+            after(QY, quantize_y, g, h, y_quads)
 
         def quantize_z(g, c, n, z_quads):
             cols = slice(P * c, P * (c + n))
@@ -254,7 +241,7 @@ def tile_microbiome_gated_growth_t2_kernel(
             )
 
         def stage_two(g, c):
-            shared = psum.tile([P, 4, P], F32, tag="mm", bufs=5, name="shared")
+            shared = psum.tile([P, 4, P], F32, tag="mm", bufs=4, name="shared")
             for t in range(4):
                 for h in range(HG):
                     nc.tensor.matmul_mx(
@@ -269,21 +256,20 @@ def tile_microbiome_gated_growth_t2_kernel(
             after(ZADD, add_y, g, c, shared)
 
         def add_y(g, c, shared):
-            if c % 2 == 0:
-                z_pair[g] = ring.tile([P, 2, P, 4], BF16, tag="z_quads", bufs=3, name="z_quads", align_bytes=64)
+            n = 1 if g == 2 and c >= 4 else ZN[g]
+            if c % n == 0:
+                z_pair[g] = ring.tile([P, 4, P, 4], BF16, tag="z_quads", bufs=3, name="z_quads", align_bytes=64)
             nc.vector.tensor_tensor(
-                out=z_pair[g][:, c % 2, :, :].rearrange("p (m i) t -> p m t i", i=4),
+                out=z_pair[g][:, c % n, :, :].rearrange("p (m i) t -> p m t i", i=4),
                 in0=shared[:].rearrange("p t (m i) -> p m t i", i=4),
                 in1=y[g][:, :, P * c : P * (c + 1)].rearrange("p t (m i) -> p m t i", i=4),
                 op=ADD,
             )
-            if g == TG - 1:
-                after(QZ, quantize_z, g, c, 1, z_pair[g][:, c % 2 : c % 2 + 1, :, :])
-            elif c % 2 == 1:
-                after(QZ, quantize_z, g, c - 1, 2, z_pair[g])
+            if c % n == n - 1:
+                after(QZ, quantize_z, g, c + 1 - n, n, z_pair[g])
 
-        def stage_three(c):
-            press = psum.tile([P, MON], F32, tag="mm", bufs=5, name="press")
+        def stage_three(c, mode):
+            press = psum.tile([P, MON], F32, tag="mm", bufs=4, name="press")
             for g in range(TG):
                 nc.tensor.matmul_mx(
                     out=press[:],
@@ -294,107 +280,106 @@ def tile_microbiome_gated_growth_t2_kernel(
                     start=(g == 0),
                     stop=(g == TG - 1),
                 )
-            after(GATE, apply_gate, c, press)
+            after(GATE, apply_gate, c, mode, press)
 
-        def apply_gate(c, press):
-            loss = ring.tile([P, MON], F32, tag="loss", bufs=3, name="loss")
-            growth = ring.tile([P, MON], F32, tag="growth", bufs=6, name="growth")
-            parts = 1 if c < HB - 1 else 2
-            engine = nc.gpsimd if c < 4 or c % 2 == 0 else nc.vector
+        def apply_gate(c, mode, press):
+            loss = ring.tile([P, MON], F32, tag="loss", bufs=3, name="loss", align_bytes=64)
+            growth = ring.tile([P, MON], F32, tag="growth", bufs=5, name="growth")
+            parts = 2 if mode == 3 else 1
             spans = [slice(MON // parts * j, MON // parts * (j + 1)) for j in range(parts)]
-            for cols in spans:
-                nc.vector.tensor_tensor(out=loss[:, cols], in0=press[:, cols], in1=gates[:, c, cols], op=MULT)
+            if mode == 2:
+                nc.scalar.copy(out=growth[:], in_=press[:])
+                nc.gpsimd.tensor_tensor(out=loss[:], in0=growth[:], in1=gates[:, c, :], op=MULT)
+            else:
+                for cols in spans:
+                    nc.vector.tensor_tensor(out=loss[:, cols], in0=press[:, cols], in1=gates[:, c, cols], op=MULT)
+            engine = nc.vector if mode in (1, 3) else nc.gpsimd
             for cols in spans:
                 engine.tensor_tensor(out=growth[:, cols], in0=rates[:, cols], in1=loss[:, cols], op=SUB)
                 nc.sync.dma_start(out=out[P * c : P * (c + 1), cols], in_=growth[:, cols])
 
         for block in (
-            (permute, 0, 0),
-            (permute, 0, 1),
-            (transpose_x, 0),
-            (permute, 0, 2),
-            (transpose_x, 1),
-            (permute, 0, 3),
-            (permute, 1, 0),
-            (transpose_x, 2),
-            (transpose_x, 3),
-            (first_stage_one, 0),
-            (first_stage_one, 1),
-            (permute, 1, 1),
-            (reorder_x, 4),
-            (permute, 1, 2),
-            (permute, 1, 3),
-            (reorder_x, 5),
-            (reorder_x, 6),
-            (first_stage_one, 2),
-            (transpose_x, 4),
-            (stage_one, 1, 0, 0),
-            (transpose_x, 5),
-            (permute, 2, 0),
-            (stage_one, 1, 0, 1),
-            (reorder_x, 7),
-            (stage_one, 1, 0, 2),
-            (transpose_x, 6),
-            (stage_one, 1, 0, 3),
-            (transpose_x, 7),
-            (stage_one, 2, 0, 0),
-            (first_stage_one, 3),
-            (stage_one, 0, 1, 0),
-            (stage_one, 0, 1, 1),
-            (stage_one, 0, 1, 2),
-            (stage_one, 1, 1, 0),
-            (permute, 2, 1),
-            (stage_one, 0, 1, 3),
-            (transpose_y, 1, 0),
-            (stage_one, 2, 1, 0),
-            (stage_one, 1, 1, 1),
-            (transpose_y, 0, 0),
-            (stage_one, 1, 1, 2),
-            (permute, 2, 2),
-            (transpose_y, 0, 1),
-            (stage_one, 1, 1, 3),
-            (permute, 2, 3),
-            (stage_one, 2, 0, 1),
-            (stage_one, 2, 1, 1),
-            (stage_one, 2, 1, 2),
-            (stage_two, 0, 0),
-            (transpose_y, 1, 1),
-            (stage_two, 0, 1),
-            (stage_one, 2, 0, 2),
-            (stage_two, 0, 2),
-            (stage_one, 2, 0, 3),
-            (stage_two, 1, 0),
-            (stage_one, 2, 1, 3),
-            (stage_two, 1, 1),
-            (stage_two, 1, 2),
-            (stage_two, 1, 3),
-            (stage_two, 0, 3),
-            (stage_two, 0, 4),
-            (transpose_y, 2, 0),
-            (stage_two, 0, 5),
-            (transpose_y, 2, 1),
-            (stage_two, 1, 4),
-            (stage_two, 0, 6),
-            (stage_two, 1, 5),
-            (stage_two, 0, 7),
-            (stage_two, 2, 0),
-            (stage_two, 2, 1),
-            (stage_two, 1, 6),
-            (stage_two, 2, 2),
-            (stage_two, 2, 3),
-            (stage_two, 2, 4),
-            (stage_three, 0),
-            (stage_two, 2, 5),
-            (stage_two, 2, 6),
-            (stage_three, 1),
-            (stage_two, 1, 7),
-            (stage_three, 2),
-            (stage_three, 3),
-            (stage_two, 2, 7),
-            (stage_three, 4),
-            (stage_three, 5),
-            (stage_three, 6),
-            (stage_three, 7),
+            (permute, 0, 2, 2,),
+            (permute, 0, 0, 2,),
+            (transpose_x, 0,),
+            (transpose_x, 1,),
+            (transpose_x, 2,),
+            (transpose_x, 3,),
+            (transpose_x, 4,),
+            (transpose_x, 5,),
+            (quantize_x, 0, 0, 2, 0, 4,),
+            (quantize_x, 0, 2, 1, 0, 4,),
+            (widen_uptake,),
+            (permute, 1, 0, 4,),
+            (reorder_x, 7,),
+            (transpose_x, 6,),
+            (stage_one_aside, 0, 0, 0,),
+            (transpose_x_words, 7,),
+            (stage_one_aside, 0, 0, 1,),
+            (stage_one, 0, 0, 2,),
+            (quantize_x, 1, 2, 1, 0, 4,),
+            (stage_one_aside, 0, 0, 3,),
+            (stage_one, 1, 0, 0,),
+            (quantize_x, 1, 0, 2, 0, 4,),
+            (stage_one, 1, 0, 1,),
+            (stage_one, 1, 0, 2,),
+            (stage_one, 1, 1, 0,),
+            (stage_one, 0, 1, 0,),
+            (stage_one, 0, 1, 1,),
+            (stage_one, 0, 1, 2,),
+            (stage_one, 1, 0, 3,),
+            (stage_one, 0, 1, 3,),
+            (permute, 2, 0, 2,),
+            (stage_one, 1, 1, 1,),
+            (stage_one, 1, 1, 2,),
+            (stage_one, 1, 1, 3,),
+            (transpose_y, 1, 0,),
+            (permute, 2, 2, 2,),
+            (transpose_y, 0, 0,),
+            (stage_one, 2, 1, 0,),
+            (stage_one, 2, 0, 0,),
+            (stage_one, 2, 1, 1,),
+            (transpose_y, 0, 1,),
+            (transpose_y, 1, 1,),
+            (stage_one, 2, 0, 1,),
+            (stage_one_aside, 2, 0, 2,),
+            (stage_one, 2, 1, 2,),
+            (stage_one_aside, 2, 1, 3,),
+            (stage_two, 0, 0,),
+            (stage_two, 1, 0,),
+            (stage_two, 0, 1,),
+            (stage_two, 0, 2,),
+            (stage_one, 2, 0, 3,),
+            (stage_two, 1, 1,),
+            (stage_two, 1, 2,),
+            (stage_two, 0, 3,),
+            (stage_two, 1, 3,),
+            (transpose_y, 2, 0,),
+            (transpose_y, 2, 1,),
+            (stage_two, 1, 4,),
+            (stage_two, 1, 5,),
+            (stage_two, 1, 6,),
+            (stage_two, 2, 0,),
+            (stage_two, 2, 1,),
+            (stage_two, 2, 2,),
+            (stage_two, 1, 7,),
+            (stage_two, 2, 3,),
+            (stage_three, 0, 2,),
+            (stage_two, 2, 4,),
+            (stage_two, 0, 4,),
+            (stage_three, 1, 0,),
+            (stage_two, 0, 5,),
+            (stage_two, 0, 6,),
+            (stage_two, 0, 7,),
+            (stage_three, 2, 0,),
+            (stage_two, 2, 5,),
+            (stage_three, 3, 0,),
+            (stage_two, 2, 6,),
+            (stage_three, 4, 0,),
+            (stage_two, 2, 7,),
+            (stage_three, 5, 0,),
+            (stage_three, 6, 3,),
+            (stage_three, 7, 3,),
         ):
             run(*block)
         for i in range(8):

from contextlib import ExitStack

import concourse.mybir as mybir
from concourse.masks import make_identity

HOSTS, TAXA, MON = 1024, 1536, 512
FLOPS = 2 * HOSTS * TAXA * TAXA + 2 * HOSTS * HOSTS * TAXA + 2 * HOSTS * TAXA * MON

F32 = mybir.dt.float32
BF16 = mybir.dt.bfloat16
U32 = mybir.dt.uint32
I32 = mybir.dt.int32
U8 = mybir.dt.uint8
E4M3 = mybir.dt.float8_e4m3fn_x4
E2M1 = mybir.dt.float4_e2m1fn_x4
ADD = mybir.AluOpType.add
MULT = mybir.AluOpType.mult
SUB = mybir.AluOpType.subtract

P = 128
LAGS = (1, 1, 3, 1, 1, 0, 7)
LOADS = (("u", 0), ("x", 0), ("x", 1), ("x", 2), ("s", 1), ("a", 0), ("x", 3), ("x", 4), ("s", 0), ("x", 5), ("x", 6), ("x", 7), ("a", 1), ("a", 2), ("s", 2))
STT, ROUND, QY, ZADD, QZ, GATE, GROUND = LAGS
COPY = mybir.ActivationFunctionType.Copy
ZN = (4, 4, 2)
K_PASS = 512
TG = TAXA // K_PASS
HG = HOSTS // K_PASS
HB = HOSTS // P


def tile_microbiome_gated_growth_t2_kernel(
    tc, x, feed_words, feed_scales, uptake, share_words, share_scales, inhib_words, inhib_scales, gate, rate, out
):
    nc = tc.nc
    with ExitStack() as ctx:
        keep = ctx.enter_context(tc.tile_pool(name="keep", bufs=1))
        ring = ctx.enter_context(tc.tile_pool(name="ring", bufs=2))
        psum = ctx.enter_context(tc.psum_pool(name="psum", bufs=4))
        ctx.enter_context(tc.manual_schedule())

        a_scale_in = [keep.tile([P, TG, K_PASS], U8, name=f"a_scale_in{g}", align_bytes=64) for g in range(TG)]
        c_scale = keep.tile([P, HG, HOSTS], U8, align_bytes=64)
        b_scale = keep.tile([P, TG, MON], U8, align_bytes=64)
        ident = keep.tile([P, P], F32)
        nc.vector.memset(a_scale_in[0][:].rearrange("p k n -> p (k n)").bitcast(I32), 0)
        make_identity(nc, ident[:])
        for g in range(1, TG):
            nc.gpsimd.memset(a_scale_in[g][:].rearrange("p k n -> p (k n)").bitcast(I32), 0)
        nc.gpsimd.memset(c_scale[:].rearrange("p k n -> p (k n)").bitcast(I32), 0)
        nc.gpsimd.memset(b_scale[:].rearrange("p k n -> p (k n)").bitcast(I32), 0)

        x_in = {}
        a_in = [keep.tile([P, TG, 2 * K_PASS], U8, name=f"a_in{g}", align_bytes=64) for g in range(TG)]
        c_codes = keep.tile([P, HG, 2 * HOSTS], U8, align_bytes=64)
        b_codes = keep.tile([P, TG, 2 * MON], U8, align_bytes=64)
        u = keep.tile([P, TG, 4], BF16, align_bytes=64)
        u_wide = keep.tile([P, TG, 4], F32, align_bytes=64)
        gates = keep.tile([P, HB, MON], BF16, align_bytes=64)
        rates = keep.tile([P, MON], BF16, align_bytes=64)

        def load_x(i):
            x_in[i] = ring.tile([P, TAXA], BF16, tag="x_in", bufs=6, name="x_in", align_bytes=64)
            nc.sync.dma_start(out=x_in[i][:], in_=x[i * P : (i + 1) * P, :])

        def load_a(g):
            cols = slice(2 * K_PASS * g, 2 * K_PASS * (g + 1))
            nc.sync.dma_start(
                out=a_in[g][:].bitcast(I32), in_=feed_words[:, :, cols].rearrange("k p b -> p k b").bitcast(I32)
            )

        def load_scales(plane, rows):
            for q in range(4):
                nc.sync.dma_start(
                    out=plane[32 * q : 32 * q + 4, :, :].bitcast(I32),
                    in_=rows[:, 4 * q : 4 * q + 4, :].rearrange("k q n -> q k n").bitcast(I32),
                )

        def load_a_scales(g):
            load_scales(a_scale_in[g], feed_scales[:, :, K_PASS * g : K_PASS * (g + 1)])

        def load_u():
            nc.sync.dma_start(out=u[:], in_=uptake.rearrange("(g p t) -> p g t", g=TG, t=4))

        for kind, i in LOADS:
            {"x": load_x, "a": load_a, "s": load_a_scales, "u": lambda i: load_u()}[kind](i)
        nc.sync.dma_start(out=c_codes[:].bitcast(I32), in_=share_words.rearrange("k p b -> p k b").bitcast(I32))
        load_scales(c_scale, share_scales)
        nc.sync.dma_start(out=b_codes[:].bitcast(I32), in_=inhib_words.rearrange("k p b -> p k b").bitcast(I32))
        load_scales(b_scale, inhib_scales)
        nc.sync.dma_start(out=gates[:], in_=gate.rearrange("(c p) n -> p c n", p=P))
        nc.sync.dma_start(out=rates[:], in_=rate.partition_broadcast(P))

        xt = [keep.tile([P, TG, K_PASS, 4], BF16, name=f"xt{h}", align_bytes=64) for h in range(HG)]
        x_codes = [keep.tile([P, TG, K_PASS], U32, name=f"x_codes{h}", align_bytes=64) for h in range(HG)]
        x_scale = [keep.tile([P, TG, K_PASS], U8, name=f"x_scale{h}", align_bytes=64) for h in range(HG)]
        a_codes = [keep.tile([P, 4, TG, 2 * P], U8, name=f"a_codes{g}", align_bytes=64) for g in range(TG)]
        a_scale = [keep.tile([P, 4, TG, P], U8, name=f"a_scale{g}", align_bytes=64) for g in range(TG)]
        y = [keep.tile([P, 4, HOSTS], F32, name=f"y{g}", align_bytes=64) for g in range(TG)]
        z_codes = [keep.tile([P, HOSTS], U32, name=f"z_codes{g}", align_bytes=64) for g in range(TG)]
        z_scale = [keep.tile([P, HOSTS], U8, name=f"z_scale{g}", align_bytes=64) for g in range(TG)]
        y_codes, y_scale, y_round = {}, {}, {}
        z_pair = {}
        x_words = {}

        work = [[] for i in range(200)]
        beat = [0]

        def after(lag, *piece):
            work[beat[0] + lag].append(piece)

        def run(block, *args):
            block(*args)
            if block in (permute, quantize_x, reorder_x, widen_uptake):
                return
            for piece in work[beat[0]]:
                piece[0](*piece[1:])
            beat[0] += 1

        def permute(g, t, n):
            nc.vector.tensor_copy(
                out=a_codes[g][:, t : t + n, :, :].rearrange("p t k (m b) -> p t (k m) b", b=2),
                in_=a_in[g][:].rearrange("p k (m t b) -> p t (k m) b", t=4, b=2)[:, t : t + n, :, :],
            )
            nc.vector.tensor_copy(
                out=a_scale[g][:, t : t + n, :, :].rearrange("p t k m -> p t (k m)"),
                in_=a_scale_in[g][:].rearrange("p k (m t) -> p t (k m)", t=4)[:, t : t + n, :],
            )

        def reorder_x(i):
            x_words[i] = ring.tile([P, 2, TG, P], F32, tag="x_words", bufs=1, name="x_words", align_bytes=64)
            nc.scalar.copy(
                out=x_words[i][:].rearrange("p s k q -> p s (k q)"),
                in_=x_in[i][:].bitcast(F32).rearrange("p (w s) -> p s w", s=2),
            )

        def transpose_x_words(i):
            transpose_x(i, True)

        def transpose_x(i, reordered=False):
            h, cols = i // 4, slice(P * (i % 4), P * (i % 4 + 1))
            words = x_in[i][:].bitcast(F32)
            for ks in ((0, 1), (2,)):
                turned = psum.tile([P, 4, P], F32, tag="tr", bufs=4, name="turned")
                for j, k in enumerate(ks):
                    for s in range(2):
                        nc.tensor.transpose(turned[:, 2 * j + s, :], x_words[i][:, s, k, :] if reordered else words[:, 256 * k + s : 256 * (k + 1) : 2], ident[:])
                nc.scalar.copy(
                    out=xt[h][:, ks[0] : ks[-1] + 1, cols, :].rearrange("p k m e -> p k (m e)").bitcast(F32).rearrange("p k (m s) -> p k m s", s=2),
                    in_=turned[:, 0 : 2 * len(ks), :].rearrange("p (k s) m -> p k m s", s=2),
                )

        def quantize_x(h, k, n, c0, cn):
            cols = slice(P * c0, P * (c0 + cn))
            codes, scale, values = x_codes[h][:, k : k + n, cols], x_scale[h][:, k : k + n, cols], xt[h][:, k : k + n, cols, :]
            nc.vector.quantize_mx(
                out=codes.rearrange("p k m -> p (k m)").bitcast(E4M3),
                scales=scale.rearrange("p k m -> p (k m)"),
                in_=values.rearrange("p k m e -> p (k m e)"),
            )


        def add_uptake(g, h, t, fed):
            hosts = slice(K_PASS * h, K_PASS * (h + 1))
            nc.vector.scalar_tensor_tensor(
                out=y[g][:, t, hosts], in0=fed[:], scalar=u[:, g, t : t + 1], in1=xt[h][:, g, :, t], op0=MULT, op1=ADD
            )
            after(ROUND, round_y, g, h, t)

        def scale_fed(g, h, t, fed):
            hosts = slice(K_PASS * h, K_PASS * (h + 1))
            scaled = ring.tile([P, K_PASS], F32, tag="loss", bufs=3, name="scaled", align_bytes=64)
            nc.scalar.activation(out=scaled[:], in_=fed[:], func=COPY, scale=u_wide[:, g, t : t + 1])
            nc.gpsimd.tensor_tensor(out=y[g][:, t, hosts], in0=scaled[:], in1=xt[h][:, g, :, t], op=ADD)
            after(GROUND, round_y, g, h, t)

        def widen_uptake():
            nc.vector.tensor_copy(out=u_wide[:], in_=u[:])

        def round_y(g, h, t):
            hosts = slice(K_PASS * h, K_PASS * (h + 1))
            nc.scalar.copy(
                out=y_round[g, h][:, t, :].rearrange("p (s q e) -> p s q e", s=2, e=2),
                in_=y[g][:, t, hosts].rearrange("p (q s e) -> p s q e", s=2, e=2),
            )

        def feed(g, h, t, fed):
            for k in range(TG):
                nc.tensor.matmul_mx(
                    out=fed[:],
                    lhsT=a_codes[g][:, t, k, :].bitcast(E2M1),
                    lhsT_scale=a_scale[g][:, t, k, :],
                    rhs=x_codes[h][:, k, :].bitcast(E4M3),
                    rhs_scale=x_scale[h][:, k, :],
                    start=(k == 0),
                    stop=(k == TG - 1),
                )

        def new_round(g, h):
            y_round[g, h] = ring.tile([P, 4, K_PASS], BF16, tag="y_round", bufs=4, name="y_round", align_bytes=64)

        def stage_one_aside(g, h, t):
            stage_one(g, h, t, True)

        def stage_one(g, h, t, aside=False):
            if t == 0:
                new_round(g, h)
            fed = psum.tile([P, K_PASS], F32, tag="mm", bufs=4, name="fed")
            feed(g, h, t, fed)
            after(STT, scale_fed if aside else add_uptake, g, h, t, fed)

        def quantize_y(g, h, y_quads):
            nc.vector.quantize_mx(
                out=y_codes[g, h][:].bitcast(E4M3),
                scales=y_scale[g, h][:],
                in_=y_quads[:].rearrange("p m e -> p (m e)"),
            )

        def transpose_y(g, h):
            y_codes[g, h] = ring.tile([P, K_PASS], U32, tag="y_codes", bufs=6, name="y_codes", align_bytes=64)
            y_scale[g, h] = ring.tile([P, K_PASS], U8, tag="y_scale", bufs=6, name="y_scale", align_bytes=64)
            y_quads = ring.tile([P, K_PASS, 4], BF16, tag="y_quads", bufs=2, name="y_quads", align_bytes=64)
            for half in range(2):
                turned = psum.tile([P, 4, P], F32, tag="tr", bufs=4, name="turned")
                for i in range(2):
                    words = y_round[g, h][:, 2 * half + i, :].bitcast(F32)
                    for s in range(2):
                        nc.tensor.transpose(turned[:, 2 * i + s, :], words[:, P * s : P * (s + 1)], ident[:])
                nc.scalar.copy(
                    out=y_quads[:, 256 * half : 256 * (half + 1), :].rearrange("p m e -> p (m e)").bitcast(F32).rearrange("p (i m s) -> p i m s", i=2, s=2),
                    in_=turned[:].rearrange("p (i s) m -> p i m s", s=2),
                )
            after(QY, quantize_y, g, h, y_quads)

        def quantize_z(g, c, n, z_quads):
            cols = slice(P * c, P * (c + n))
            nc.vector.quantize_mx(
                out=z_codes[g][:, cols].bitcast(E4M3),
                scales=z_scale[g][:, cols],
                in_=z_quads[:, 0:n, :, :].rearrange("p c m e -> p (c m e)"),
            )

        def stage_two(g, c):
            shared = psum.tile([P, 4, P], F32, tag="mm", bufs=4, name="shared")
            for t in range(4):
                for h in range(HG):
                    nc.tensor.matmul_mx(
                        out=shared[:, t, :],
                        lhsT=y_codes[g, h][:, P * t : P * (t + 1)].bitcast(E4M3),
                        lhsT_scale=y_scale[g, h][:, P * t : P * (t + 1)],
                        rhs=c_codes[:, h, 256 * c : 256 * (c + 1)].bitcast(E2M1),
                        rhs_scale=c_scale[:, h, P * c : P * (c + 1)],
                        start=(h == 0),
                        stop=(h == HG - 1),
                    )
            after(ZADD, add_y, g, c, shared)

        def add_y(g, c, shared):
            n = 1 if g == 2 and c >= 4 else ZN[g]
            if c % n == 0:
                z_pair[g] = ring.tile([P, 4, P, 4], BF16, tag="z_quads", bufs=3, name="z_quads", align_bytes=64)
            nc.vector.tensor_tensor(
                out=z_pair[g][:, c % n, :, :].rearrange("p (m i) t -> p m t i", i=4),
                in0=shared[:].rearrange("p t (m i) -> p m t i", i=4),
                in1=y[g][:, :, P * c : P * (c + 1)].rearrange("p t (m i) -> p m t i", i=4),
                op=ADD,
            )
            if c % n == n - 1:
                after(QZ, quantize_z, g, c + 1 - n, n, z_pair[g])

        def stage_three(c, mode):
            press = psum.tile([P, MON], F32, tag="mm", bufs=4, name="press")
            for g in range(TG):
                nc.tensor.matmul_mx(
                    out=press[:],
                    lhsT=z_codes[g][:, P * c : P * (c + 1)].bitcast(E4M3),
                    lhsT_scale=z_scale[g][:, P * c : P * (c + 1)],
                    rhs=b_codes[:, g, :].bitcast(E2M1),
                    rhs_scale=b_scale[:, g, :],
                    start=(g == 0),
                    stop=(g == TG - 1),
                )
            after(GATE, apply_gate, c, mode, press)

        def apply_gate(c, mode, press):
            loss = ring.tile([P, MON], F32, tag="loss", bufs=3, name="loss", align_bytes=64)
            growth = ring.tile([P, MON], F32, tag="growth", bufs=5, name="growth")
            parts = 2 if mode == 3 else 1
            spans = [slice(MON // parts * j, MON // parts * (j + 1)) for j in range(parts)]
            if mode == 2:
                nc.scalar.copy(out=growth[:], in_=press[:])
                nc.gpsimd.tensor_tensor(out=loss[:], in0=growth[:], in1=gates[:, c, :], op=MULT)
            else:
                for cols in spans:
                    nc.vector.tensor_tensor(out=loss[:, cols], in0=press[:, cols], in1=gates[:, c, cols], op=MULT)
            engine = nc.vector if mode in (1, 3) else nc.gpsimd
            for cols in spans:
                engine.tensor_tensor(out=growth[:, cols], in0=rates[:, cols], in1=loss[:, cols], op=SUB)
                nc.sync.dma_start(out=out[P * c : P * (c + 1), cols], in_=growth[:, cols])

        for block in (
            (permute, 0, 2, 2,),
            (permute, 0, 0, 2,),
            (transpose_x, 0,),
            (transpose_x, 1,),
            (transpose_x, 2,),
            (transpose_x, 3,),
            (transpose_x, 4,),
            (transpose_x, 5,),
            (quantize_x, 0, 0, 2, 0, 4,),
            (quantize_x, 0, 2, 1, 0, 4,),
            (widen_uptake,),
            (permute, 1, 0, 4,),
            (reorder_x, 7,),
            (transpose_x, 6,),
            (stage_one_aside, 0, 0, 0,),
            (transpose_x_words, 7,),
            (stage_one_aside, 0, 0, 1,),
            (stage_one, 0, 0, 2,),
            (quantize_x, 1, 2, 1, 0, 4,),
            (stage_one_aside, 0, 0, 3,),
            (stage_one, 1, 0, 0,),
            (quantize_x, 1, 0, 2, 0, 4,),
            (stage_one, 1, 0, 1,),
            (stage_one, 1, 0, 2,),
            (stage_one, 1, 1, 0,),
            (stage_one, 0, 1, 0,),
            (stage_one, 0, 1, 1,),
            (stage_one, 0, 1, 2,),
            (stage_one, 1, 0, 3,),
            (stage_one, 0, 1, 3,),
            (permute, 2, 0, 2,),
            (stage_one, 1, 1, 1,),
            (stage_one, 1, 1, 2,),
            (stage_one, 1, 1, 3,),
            (transpose_y, 1, 0,),
            (permute, 2, 2, 2,),
            (transpose_y, 0, 0,),
            (stage_one, 2, 1, 0,),
            (stage_one, 2, 0, 0,),
            (stage_one, 2, 1, 1,),
            (transpose_y, 0, 1,),
            (transpose_y, 1, 1,),
            (stage_one, 2, 0, 1,),
            (stage_one_aside, 2, 0, 2,),
            (stage_one, 2, 1, 2,),
            (stage_one_aside, 2, 1, 3,),
            (stage_two, 0, 0,),
            (stage_two, 1, 0,),
            (stage_two, 0, 1,),
            (stage_two, 0, 2,),
            (stage_one, 2, 0, 3,),
            (stage_two, 1, 1,),
            (stage_two, 1, 2,),
            (stage_two, 0, 3,),
            (stage_two, 1, 3,),
            (transpose_y, 2, 0,),
            (transpose_y, 2, 1,),
            (stage_two, 1, 4,),
            (stage_two, 1, 5,),
            (stage_two, 1, 6,),
            (stage_two, 2, 0,),
            (stage_two, 2, 1,),
            (stage_two, 2, 2,),
            (stage_two, 1, 7,),
            (stage_two, 2, 3,),
            (stage_three, 0, 2,),
            (stage_two, 2, 4,),
            (stage_two, 0, 4,),
            (stage_three, 1, 0,),
            (stage_two, 0, 5,),
            (stage_two, 0, 6,),
            (stage_two, 0, 7,),
            (stage_three, 2, 0,),
            (stage_two, 2, 5,),
            (stage_three, 3, 0,),
            (stage_two, 2, 6,),
            (stage_three, 4, 0,),
            (stage_two, 2, 7,),
            (stage_three, 5, 0,),
            (stage_three, 6, 3,),
            (stage_three, 7, 3,),
        ):
            run(*block)
        for i in range(8):
            run(len, ())
